import numpy as np
import ml_dtypes


def mxq(x, axis, fmt="e4m3"):
    dtype, down = {"e4m3": (ml_dtypes.float8_e4m3fn, 7), "e5m2": (ml_dtypes.float8_e5m2, 14)}[fmt]
    v = np.moveaxis(np.asarray(x, np.float32).astype(ml_dtypes.bfloat16).astype(np.float64), axis, -1)
    blocks = v.reshape(v.shape[:-1] + (-1, 32))
    amax = np.abs(blocks).max(-1, keepdims=True)
    byte = np.maximum(np.where(amax > 0, np.frexp(amax)[1] - 1 + 127, 0) - down, 1)
    scale = np.exp2(byte - 127.0)
    codes = (blocks / scale).astype(np.float32).astype(dtype).astype(np.float64)
    return np.moveaxis((codes * scale).reshape(v.shape), -1, axis)


WIDE = False


def mx_kscale(k):
    if not WIDE:
        return np.ones(k)
    levels = np.array([10, -10, 5, -5, 0])
    if k % 512:
        return np.exp2(np.random.permutation(np.resize(levels, k // 32))).repeat(32)
    a = np.empty((k // 512, 16))
    for p in range(k // 512):
        a[p, :8] = np.random.permutation(np.resize(levels, 8))
        for g in range(8):
            far = levels[np.abs(levels - a[p, g]) >= 10]
            a[p, g + 8] = far[np.random.randint(len(far))]
    return np.exp2(a.ravel()).repeat(32)


def f64(x):
    return np.asarray(x).astype(np.float64)


def striped(idx):
    return np.tile(np.asarray(idx).reshape(-1, 16).T, (8, 1)).astype(np.uint16)


def unstriped(offs):
    return offs[:16].T.reshape(-1).astype(np.int64)


E2M1 = np.array([0.0, 0.5, 1.0, 1.5, 2.0, 3.0, 4.0, 6.0, -0.0, -0.5, -1.0, -1.5, -2.0, -3.0, -4.0, -6.0])


def pack_weight(w, fmt):
    k, n = w.shape
    w = f64(np.asarray(w, np.float32).astype(ml_dtypes.bfloat16)).reshape(k // 32, 32, n)
    amax = np.abs(w).max(1)
    if fmt == "e4m3":
        byte = np.frexp(amax)[1] - 1 + 127 - 7
    else:
        mant, ex = np.frexp(amax / 6.0)
        byte = np.where(mant > 0.5, ex, ex - 1) + 127
    byte = np.clip(np.where(amax > 0, byte, 1), 1, 254)
    scaled = (w * np.exp2(127.0 - byte)[:, None, :]).reshape(k, n).astype(np.float32)
    by_word = np.ascontiguousarray(scaled.reshape(k // 512, 128, 4, n).transpose(0, 1, 3, 2))
    if fmt == "e4m3":
        words = by_word.astype(ml_dtypes.float8_e4m3fn).view(np.uint8)
    else:
        c = by_word.astype(ml_dtypes.float4_e2m1fn).view(np.uint8) & 0xF
        words = (c[..., 0::2] | (c[..., 1::2] << 4)).reshape(k // 512, 128, 2 * n)
    return np.ascontiguousarray(words), np.ascontiguousarray(byte.astype(np.uint8).reshape(k // 512, 16, n))


def unpack_weight(words, scales, fmt):
    g, _, n = scales.shape
    words = np.ascontiguousarray(words).reshape(g, 128, n, -1)
    if fmt == "e4m3":
        vals = words.view(ml_dtypes.float8_e4m3fn).astype(np.float64)
    else:
        nib = np.empty((g, 128, n, 4), np.uint8)
        nib[..., 0::2] = words & 0xF
        nib[..., 1::2] = words >> 4
        vals = E2M1[nib]
    vals = vals * np.repeat(np.exp2(scales.astype(np.float64) - 127.0), 8, axis=1)[..., None]
    return vals.transpose(0, 1, 3, 2).reshape(g * 512, n)


D, E, T, I, Q = 512, 512, 2048, 512, 128


def setup_inputs():
    n = np.random.standard_normal
    idx2 = np.random.permutation(I)[:I]
    idx = np.random.permutation(T)[:I]
    fd = mx_kscale(D)
    fe = mx_kscale(E)
    keysp = pack_weight(n((D, T)) / fd[:, None], "e4m3")
    valsp = pack_weight(n((E, T)) / fe[:, None], "e4m3")
    return {
        "query": (n((D, Q)) * 0.7 / np.sqrt(D) * fd[:, None]).astype(np.float32),
        "keys_words": keysp[0],
        "keys_scales": keysp[1],
        "gout": (n((E, Q)) * 1 / np.sqrt(E) * fe[:, None]).astype(np.float32),
        "vals_words": valsp[0],
        "vals_scales": valsp[1],
        "dquery": (n((D, Q)) * 1.0 / np.sqrt(D) * fd[:, None]).astype(np.float32),
        "base": (0.5 * n((Q, T))).astype(np.float32),
        "offs2": striped(idx2),
        "offs": striped(idx),
    }


def reference(query, keys_words, keys_scales, gout, vals_words, vals_scales, dquery, base, offs2, offs):
    idx2 = unstriped(offs2)
    idx = unstriped(offs)
    keysu = unpack_weight(keys_words, keys_scales, "e4m3")
    valsu = unpack_weight(vals_words, vals_scales, "e4m3")
    queryq = mxq(f64(query), 0, "e4m3")
    keysidxg = keysu[:, idx]
    a = queryq.T @ keysidxg
    dqueryq = mxq(f64(dquery), 0, "e4m3")
    ta = dqueryq.T @ keysidxg
    pa = np.exp(a)
    pb = np.sqrt(pa)
    p = pa * pb[:, idx2]
    z = np.sum(p, axis=1, keepdims=True)
    goutq = mxq(f64(gout), 0, "e4m3")
    valsidxg = valsu[:, idx]
    c0 = goutq.T @ valsidxg
    dz = np.sum(c0 * p / np.square(z) * (-1.0), axis=1, keepdims=True)
    dp = c0 / z + dz
    e1 = dp * pa
    s1 = np.zeros((Q, I))
    s1[:, idx2] = e1
    dpa = dp * pb[:, idx2] + s1 * 0.5 / np.sqrt(pa)
    tpa = ta * pa
    tpb = tpa * 0.5 / pb
    tp = tpa * pb[:, idx2] + tpb[:, idx2] * pa
    tz = np.sum(tp, axis=1, keepdims=True)
    tdz = np.sum((tp * c0 - tz * z * 2.0 * c0 * p / np.square(z)) / np.square(z) * (-1.0), axis=1, keepdims=True)
    tdp = tz * c0 / np.square(z) * (-1.0) + tdz
    te1 = tdp * pa + tpa * dp
    ts1 = np.zeros((Q, I))
    ts1[:, idx2] = te1
    tdpa = tdp * pb[:, idx2] + tpb[:, idx2] * dp + (ts1 * 0.5 - tpa * 0.5 / np.sqrt(pa) * s1 * 0.5 / np.sqrt(pa)) / np.sqrt(pa)
    tda = tdpa * pa + tpa * dpa
    gs = tda * 512.0
    gf = np.zeros((Q, T))
    gf[:, idx] = gs
    y = f64(base) + gf
    return y

@@ -1,0 +1,186 @@
+from contextlib import ExitStack
+
+import concourse.mybir as mybir
+
+D, E, T, I, Q = 512, 512, 2048, 512, 128
+FLOPS = 3 * 2 * 512 * Q * I
+
+F32 = mybir.dt.float32
+BF16 = mybir.dt.bfloat16
+I32 = mybir.dt.int32
+U32 = mybir.dt.uint32
+U16 = mybir.dt.uint16
+U8 = mybir.dt.uint8
+FP8X4 = mybir.dt.float8_e4m3fn_x4
+ALU = mybir.AluOpType
+ACT = mybir.ActivationFunctionType
+
+P = 128
+PACK = 4
+LOOKUP_COLS = I + 16
+LINK_COLS = 704
+OUT_CHUNK = 512
+
+
+def tile_attend_hvlinkedproduct_s_kernel(
+    tc, query, keys_words, keys_scales, gout, vals_words, vals_scales, dquery, base, offs2, offs, out
+):
+    nc = tc.nc
+    with ExitStack() as ctx:
+        lists = ctx.enter_context(tc.tile_pool(name="lists", bufs=1))
+        sb = ctx.enter_context(tc.tile_pool(name="sb", bufs=1))
+        ps = ctx.enter_context(tc.psum_pool(name="ps", bufs=1))
+
+        token_list = lists.tile([P, I // 16], U16, name="token_list")
+        link_list = lists.tile([P, I // 16], U16, name="link_list")
+
+        def wide(name, cols=I, dtype=F32, tag=None):
+            return sb.tile([P, cols], dtype, name=name, tag=tag or name, align_bytes=64)
+
+        def column(name):
+            return sb.tile([P, 1], F32, name=name, align_bytes=64)
+
+        key_bytes = wide("key_bytes", T, U8, tag="first_big")
+        val_bytes = wide("val_bytes", T, U8)
+        key_words = wide("key_words", T, I32, tag="second_big")
+        placed = wide("placed", T)
+        pb = wide("pb", LOOKUP_COLS)
+        tpb = wide("tpb", LOOKUP_COLS)
+
+        nc.vector.memset(key_bytes[:].bitcast(I32), 0)
+        nc.vector.memset(val_bytes[:].bitcast(I32), 0)
+        nc.vector.memset(pb[:, I:], 0.0)
+        nc.vector.memset(tpb[:, I:], 0.0)
+        nc.vector.memset(placed[:], 0.0)
+
+        def load_scale_rows(queue, tile, rows):
+            for quad in range(4):
+                queue.dma_start(
+                    out=tile[32 * quad : 32 * quad + 4, :].bitcast(I32),
+                    in_=rows[0, 4 * quad : 4 * quad + 4, :].bitcast(I32),
+                )
+
+        def load_words(tile, words):
+            nc.sync.dma_start(out=tile[:], in_=words[0].rearrange("p n t -> p (n t)").bitcast(I32))
+
+        def load_rows(name, rows, tag):
+            raw = sb.tile([P, PACK, Q], F32, name=name, tag=tag, align_bytes=64)
+            nc.sync.dma_start(out=raw[:], in_=rows.rearrange("(p j) w -> p j w", j=PACK))
+            return raw
+
+        nc.sync.dma_start(token_list[:], offs)
+        load_scale_rows(nc.scalar, key_bytes, keys_scales)
+        nc.sync.dma_start(link_list[:], offs2)
+        query_raw = load_rows("query_raw", query, "raw_a")
+        load_words(key_words, keys_words)
+        dquery_raw = load_rows("dquery_raw", dquery, "raw_b")
+        load_scale_rows(nc.sync, val_bytes, vals_scales)
+
+        def interleave(name, raw):
+            grouped = sb.tile([P, Q, PACK], BF16, name=name + "_bf16", align_bytes=64)
+            nc.scalar.copy(out=grouped[:], in_=raw[:].rearrange("p j w -> p w j"))
+            return grouped
+
+        query_bf16 = interleave("query", query_raw)
+        dquery_bf16 = interleave("dquery", dquery_raw)
+        gout_bf16 = interleave("gout", load_rows("gout_raw", gout, "raw_a"))
+
+        def quantise(name, grouped):
+            codes = wide(name + "_codes", Q, U32)
+            scales = wide(name + "_scales", Q, U8)
+            nc.vector.quantize_mx(
+                out=codes[:].bitcast(FP8X4), scales=scales[:], in_=grouped[:].rearrange("p w j -> p (w j)")
+            )
+            return codes, scales
+
+        def gather_bytes(name, tile):
+            got = wide(name, I, U8)
+            nc.vector.tensor_copy(got[:], tile[:].indirect(token_list[:]))
+            return got
+
+        def gather_words(name, tile):
+            got = wide(name, I, U32)
+            nc.vector.tensor_copy(got[:], tile[:].bitcast(U32).indirect(token_list[:]))
+            return got
+
+        def product(name, stationary, words, scale_bytes):
+            bank = ps.tile([P, I], F32, name=name)
+            nc.tensor.matmul_mx(
+                out=bank[:],
+                lhsT=stationary[0][:].bitcast(FP8X4),
+                lhsT_scale=stationary[1][:],
+                rhs=words[:].bitcast(FP8X4),
+                rhs_scale=scale_bytes[:],
+                start=True,
+                stop=True,
+            )
+            return bank
+
+        slot_key_bytes = gather_bytes("slot_key_bytes", key_bytes)
+        val_words = wide("val_words", T, I32, tag="first_big")
+        load_words(val_words, vals_words)
+        query_mx = quantise("query", query_bf16)
+        slot_key_words = gather_words("slot_key_words", key_words)
+        base_sb = wide("base_sb", T, tag="second_big")
+        nc.sync.dma_start(out=base_sb[:], in_=base)
+        a = product("a", query_mx, slot_key_words, slot_key_bytes)
+        dquery_mx = quantise("dquery", dquery_bf16)
+        ta = product("ta", dquery_mx, slot_key_words, slot_key_bytes)
+
+        unused = wide("unused")
+        shift = column("shift")
+        nc.vector.tensor_scalar(unused[:], a[:], -0.5, None, ALU.mult, ALU.min, accum_out=shift[:])
+        nc.scalar.activation(pb[:, :I], a[:], ACT.Exp, bias=shift[:], scale=0.5)
+        pa = wide("pa")
+        nc.scalar.activation(pa[:], pb[:, :I], ACT.Square)
+
+        slot_val_bytes = gather_bytes("slot_val_bytes", val_bytes)
+
+        nc.vector.scalar_tensor_tensor(tpb[:, :I], ta[:], 0.5, pb[:, :I], ALU.mult, ALU.mult)
+        p = wide("p")
+        nc.vector.tensor_tensor(p[:], pb[:].indirect(link_list[:]), pa[:], ALU.mult)
+        minus_p = wide("minus_p")
+        minus_z = column("minus_z")
+        nc.scalar.activation(minus_p[:], p[:], ACT.Copy, scale=-1.0, accum_out=minus_z[:])
+        linked = wide("linked")
+        nc.vector.tensor_tensor(linked[:], tpb[:].indirect(link_list[:]), pa[:], ALU.mult)
+        slot_val_words = gather_words("slot_val_words", val_words)
+        gout_mx = quantise("gout", gout_bf16)
+        c0 = product("c0", gout_mx, slot_val_words, slot_val_bytes)
+        minus_rz = column("minus_rz")
+        nc.vector.reciprocal(minus_rz[:], minus_z[:])
+        gain = column("gain")
+        nc.scalar.activation(gain[:], minus_rz[:], ACT.Copy, scale=-256.0)
+        minus_w = wide("minus_w")
+        nc.scalar.activation(minus_w[:], p[:], ACT.Copy, scale=minus_rz[:])
+
+        own = wide("own")
+        nc.vector.scalar_tensor_tensor(own[:], ta[:], gain[:], p[:], ALU.mult, ALU.mult)
+        tw = wide("tw")
+        tw_sum = column("tw_sum")
+        nc.vector.scalar_tensor_tensor(tw[:], linked[:], gain[:], own[:], ALU.mult, ALU.add, accum_out=tw_sum[:])
+        weighted = wide("weighted")
+        minus_mean = column("minus_mean")
+        nc.vector.scalar_tensor_tensor(
+            weighted[:], c0[:], minus_rz[:], p[:], ALU.mult, ALU.mult, accum_out=minus_mean[:]
+        )
+        v = wide("v")
+        nc.vector.scalar_tensor_tensor(v[:], minus_w[:], tw_sum[:], tw[:], ALU.mult, ALU.add)
+        cv = wide("cv")
+        cv_sum = column("cv_sum")
+        nc.vector.scalar_tensor_tensor(cv[:], c0[:], minus_mean[:], v[:], ALU.add, ALU.mult, accum_out=cv_sum[:])
+        u = wide("u")
+        nc.vector.scalar_tensor_tensor(u[:], minus_w[:], cv_sum[:], cv[:], ALU.mult, ALU.add)
+
+        sent = wide("sent", LINK_COLS)
+        nc.vector.tensor_copy(sent[:].indirect(link_list[:]), u[:])
+        twice_u = wide("twice_u")
+        nc.scalar.activation(twice_u[:], u[:], ACT.Copy, scale=2.0)
+        nc.vector.tensor_tensor(placed[:].indirect(token_list[:]), twice_u[:], sent[:, :I], ALU.add)
+
+        for k in range(T // OUT_CHUNK):
+            cols = slice(k * OUT_CHUNK, (k + 1) * OUT_CHUNK)
+            result = wide("result%d" % k, OUT_CHUNK)
+            nc.vector.tensor_tensor(result[:], placed[:, cols], base_sb[:, cols], ALU.add)
+            queue = nc.sync if k % 2 == 0 else nc.scalar
+            queue.dma_start(out=out[:, cols], in_=result[:])

@@ -19,7 +19,7 @@ P = 128
 PACK = 4
 LOOKUP_COLS = I + 16
 LINK_COLS = 704
-OUT_CHUNK = 512
+OUT_EDGES = (0, 256, 768, 1280, 1792, 2048)
 
 
 def tile_attend_hvlinkedproduct_s_kernel(
@@ -29,6 +29,7 @@ def tile_attend_hvlinkedproduct_s_kernel(
     with ExitStack() as ctx:
         lists = ctx.enter_context(tc.tile_pool(name="lists", bufs=1))
         sb = ctx.enter_context(tc.tile_pool(name="sb", bufs=1))
+        shared = ctx.enter_context(tc.tile_pool(name="shared", bufs=1))
         ps = ctx.enter_context(tc.psum_pool(name="ps", bufs=1))
 
         token_list = lists.tile([P, I // 16], U16, name="token_list")
@@ -37,25 +38,26 @@ def tile_attend_hvlinkedproduct_s_kernel(
         def wide(name, cols=I, dtype=F32, tag=None):
             return sb.tile([P, cols], dtype, name=name, tag=tag or name, align_bytes=64)
 
-        def column(name):
-            return sb.tile([P, 1], F32, name=name, align_bytes=64)
+        def column(name, tag=None):
+            return sb.tile([P, 1], F32, name=name, tag=tag or name, align_bytes=64)
 
-        key_bytes = wide("key_bytes", T, U8, tag="first_big")
+        def overlaid(name, shape, dtype, offset):
+            return shared.tile(shape, dtype, name=name, offset=offset, align_bytes=64)
+
+        key_bytes = wide("key_bytes", T, U8)
         val_bytes = wide("val_bytes", T, U8)
-        key_words = wide("key_words", T, I32, tag="second_big")
+        key_words = wide("key_words", T, I32)
         placed = wide("placed", T)
         pb = wide("pb", LOOKUP_COLS)
-        tpb = wide("tpb", LOOKUP_COLS)
 
         nc.vector.memset(key_bytes[:].bitcast(I32), 0)
-        nc.vector.memset(val_bytes[:].bitcast(I32), 0)
         nc.vector.memset(pb[:, I:], 0.0)
-        nc.vector.memset(tpb[:, I:], 0.0)
         nc.vector.memset(placed[:], 0.0)
+        nc.vector.memset(val_bytes[:].bitcast(I32), 0)
 
-        def load_scale_rows(queue, tile, rows):
+        def load_scale_rows(tile, rows):
             for quad in range(4):
-                queue.dma_start(
+                nc.sync.dma_start(
                     out=tile[32 * quad : 32 * quad + 4, :].bitcast(I32),
                     in_=rows[0, 4 * quad : 4 * quad + 4, :].bitcast(I32),
                 )
@@ -63,27 +65,13 @@ def tile_attend_hvlinkedproduct_s_kernel(
         def load_words(tile, words):
             nc.sync.dma_start(out=tile[:], in_=words[0].rearrange("p n t -> p (n t)").bitcast(I32))
 
-        def load_rows(name, rows, tag):
-            raw = sb.tile([P, PACK, Q], F32, name=name, tag=tag, align_bytes=64)
+        def load_rows(raw, rows):
             nc.sync.dma_start(out=raw[:], in_=rows.rearrange("(p j) w -> p j w", j=PACK))
-            return raw
 
-        nc.sync.dma_start(token_list[:], offs)
-        load_scale_rows(nc.scalar, key_bytes, keys_scales)
-        nc.sync.dma_start(link_list[:], offs2)
-        query_raw = load_rows("query_raw", query, "raw_a")
-        load_words(key_words, keys_words)
-        dquery_raw = load_rows("dquery_raw", dquery, "raw_b")
-        load_scale_rows(nc.sync, val_bytes, vals_scales)
-
-        def interleave(name, raw):
-            grouped = sb.tile([P, Q, PACK], BF16, name=name + "_bf16", align_bytes=64)
+        def interleave(name, raw, tag):
+            grouped = sb.tile([P, Q, PACK], BF16, name=name + "_bf16", tag=tag, align_bytes=64)
             nc.scalar.copy(out=grouped[:], in_=raw[:].rearrange("p j w -> p w j"))
             return grouped
-
-        query_bf16 = interleave("query", query_raw)
-        dquery_bf16 = interleave("dquery", dquery_raw)
-        gout_bf16 = interleave("gout", load_rows("gout_raw", gout, "raw_a"))
 
         def quantise(name, grouped):
             codes = wide(name + "_codes", Q, U32)
@@ -93,14 +81,9 @@ def tile_attend_hvlinkedproduct_s_kernel(
             )
             return codes, scales
 
-        def gather_bytes(name, tile):
-            got = wide(name, I, U8)
-            nc.vector.tensor_copy(got[:], tile[:].indirect(token_list[:]))
-            return got
-
-        def gather_words(name, tile):
-            got = wide(name, I, U32)
-            nc.vector.tensor_copy(got[:], tile[:].bitcast(U32).indirect(token_list[:]))
+        def gather(name, window):
+            got = wide(name, I, window.dtype)
+            nc.vector.tensor_copy(got[:], window.indirect(token_list[:]))
             return got
 
         def product(name, stationary, words, scale_bytes):
@@ -116,56 +99,74 @@ def tile_attend_hvlinkedproduct_s_kernel(
             )
             return bank
 
-        slot_key_bytes = gather_bytes("slot_key_bytes", key_bytes)
-        val_words = wide("val_words", T, I32, tag="first_big")
+        nc.sync.dma_start(token_list[:], offs)
+        nc.sync.dma_start(link_list[:], offs2)
+        query_raw = overlaid("query_raw", [P, PACK, Q], F32, 0)
+        load_rows(query_raw, query)
+        load_scale_rows(key_bytes, keys_scales)
+        load_words(key_words, keys_words)
+        dquery_raw = sb.tile([P, PACK, Q], F32, name="dquery_raw", tag="dquery_raw", align_bytes=64)
+        load_rows(dquery_raw, dquery)
+        load_scale_rows(val_bytes, vals_scales)
+
+        query_bf16 = interleave("query", query_raw, "query_bf16")
+        val_words = overlaid("val_words", [P, T], I32, 0)
         load_words(val_words, vals_words)
+        dquery_bf16 = interleave("dquery", dquery_raw, "dquery_bf16")
+
+        slot_key_bytes = gather("slot_key_bytes", key_bytes[:])
+        gout_raw = sb.tile([P, PACK, Q], F32, name="gout_raw", tag="key_bytes", align_bytes=64)
+        load_rows(gout_raw, gout)
         query_mx = quantise("query", query_bf16)
-        slot_key_words = gather_words("slot_key_words", key_words)
-        base_sb = wide("base_sb", T, tag="second_big")
-        nc.sync.dma_start(out=base_sb[:], in_=base)
+        slot_key_words = gather("slot_key_words", key_words[:].bitcast(U32))
         a = product("a", query_mx, slot_key_words, slot_key_bytes)
+        slot_val_bytes = gather("slot_val_bytes", val_bytes[:])
         dquery_mx = quantise("dquery", dquery_bf16)
         ta = product("ta", dquery_mx, slot_key_words, slot_key_bytes)
 
-        unused = wide("unused")
-        shift = column("shift")
+        unused = wide("unused", tag="val_bytes")
+        shift = column("shift", "dquery_raw")
         nc.vector.tensor_scalar(unused[:], a[:], -0.5, None, ALU.mult, ALU.min, accum_out=shift[:])
         nc.scalar.activation(pb[:, :I], a[:], ACT.Exp, bias=shift[:], scale=0.5)
         pa = wide("pa")
         nc.scalar.activation(pa[:], pb[:, :I], ACT.Square)
+        gout_bf16 = interleave("gout", gout_raw, "val_bytes")
 
-        slot_val_bytes = gather_bytes("slot_val_bytes", val_bytes)
-
-        nc.vector.scalar_tensor_tensor(tpb[:, :I], ta[:], 0.5, pb[:, :I], ALU.mult, ALU.mult)
-        p = wide("p")
+        slot_val_words = gather("slot_val_words", val_words[:].bitcast(U32))
+        p = overlaid("p", [P, I], F32, 0)
         nc.vector.tensor_tensor(p[:], pb[:].indirect(link_list[:]), pa[:], ALU.mult)
         minus_p = wide("minus_p")
         minus_z = column("minus_z")
         nc.scalar.activation(minus_p[:], p[:], ACT.Copy, scale=-1.0, accum_out=minus_z[:])
-        linked = wide("linked")
-        nc.vector.tensor_tensor(linked[:], tpb[:].indirect(link_list[:]), pa[:], ALU.mult)
-        slot_val_words = gather_words("slot_val_words", val_words)
         gout_mx = quantise("gout", gout_bf16)
         c0 = product("c0", gout_mx, slot_val_words, slot_val_bytes)
+
+        tpb = overlaid("tpb", [P, LOOKUP_COLS], F32, 4 * I)
+        nc.vector.memset(tpb[:, I:], 0.0)
+        nc.vector.scalar_tensor_tensor(tpb[:, :I], ta[:], 0.5, pb[:, :I], ALU.mult, ALU.mult)
+        own = wide("own")
+        nc.vector.tensor_tensor(own[:], ta[:], p[:], ALU.mult)
+        linked = wide("linked", tag="val_bytes")
+        nc.vector.tensor_tensor(linked[:], tpb[:].indirect(link_list[:]), pa[:], ALU.mult)
         minus_rz = column("minus_rz")
         nc.vector.reciprocal(minus_rz[:], minus_z[:])
-        gain = column("gain")
-        nc.scalar.activation(gain[:], minus_rz[:], ACT.Copy, scale=-256.0)
         minus_w = wide("minus_w")
         nc.scalar.activation(minus_w[:], p[:], ACT.Copy, scale=minus_rz[:])
+        gain = column("gain")
+        nc.scalar.activation(gain[:], minus_rz[:], ACT.Copy, scale=-256.0)
 
-        own = wide("own")
-        nc.vector.scalar_tensor_tensor(own[:], ta[:], gain[:], p[:], ALU.mult, ALU.mult)
-        tw = wide("tw")
-        tw_sum = column("tw_sum")
-        nc.vector.scalar_tensor_tensor(tw[:], linked[:], gain[:], own[:], ALU.mult, ALU.add, accum_out=tw_sum[:])
+        tp = wide("tp")
+        tz = column("tz")
+        nc.vector.scalar_tensor_tensor(tp[:], linked[:], 1.0, own[:], ALU.mult, ALU.add, accum_out=tz[:])
         weighted = wide("weighted")
         minus_mean = column("minus_mean")
         nc.vector.scalar_tensor_tensor(
             weighted[:], c0[:], minus_rz[:], p[:], ALU.mult, ALU.mult, accum_out=minus_mean[:]
         )
+        base_sb = overlaid("base_sb", [P, T], F32, 0)
+        nc.sync.dma_start(out=base_sb[:], in_=base)
         v = wide("v")
-        nc.vector.scalar_tensor_tensor(v[:], minus_w[:], tw_sum[:], tw[:], ALU.mult, ALU.add)
+        nc.vector.scalar_tensor_tensor(v[:], minus_w[:], tz[:], tp[:], ALU.mult, ALU.add)
         cv = wide("cv")
         cv_sum = column("cv_sum")
         nc.vector.scalar_tensor_tensor(cv[:], c0[:], minus_mean[:], v[:], ALU.add, ALU.mult, accum_out=cv_sum[:])
@@ -178,9 +179,9 @@ def tile_attend_hvlinkedproduct_s_kernel(
         nc.scalar.activation(twice_u[:], u[:], ACT.Copy, scale=2.0)
         nc.vector.tensor_tensor(placed[:].indirect(token_list[:]), twice_u[:], sent[:, :I], ALU.add)
 
-        for k in range(T // OUT_CHUNK):
-            cols = slice(k * OUT_CHUNK, (k + 1) * OUT_CHUNK)
-            result = wide("result%d" % k, OUT_CHUNK)
-            nc.vector.tensor_tensor(result[:], placed[:, cols], base_sb[:, cols], ALU.add)
+        for k in range(len(OUT_EDGES) - 1):
+            cols = slice(OUT_EDGES[k], OUT_EDGES[k + 1])
+            result = wide("result%d" % k, cols.stop - cols.start)
+            nc.vector.scalar_tensor_tensor(result[:], placed[:, cols], gain[:], base_sb[:, cols], ALU.mult, ALU.add)
             queue = nc.sync if k % 2 == 0 else nc.scalar
             queue.dma_start(out=out[:, cols], in_=result[:])

@@ -1,6 +1,7 @@
 from contextlib import ExitStack
 
 import concourse.mybir as mybir
+from concourse.masks import make_identity
 
 D, E, T, I, Q = 512, 512, 2048, 512, 128
 FLOPS = 3 * 2 * 512 * Q * I
@@ -18,7 +19,7 @@ ACT = mybir.ActivationFunctionType
 P = 128
 PACK = 4
 LOOKUP_COLS = I + 16
-LINK_COLS = 704
+LINK_COLS = 2 * I
 OUT_EDGES = (0, 256, 768, 1280, 1792, 2048)
 
 
@@ -49,6 +50,9 @@ def tile_attend_hvlinkedproduct_s_kernel(
         key_words = wide("key_words", T, I32)
         placed = wide("placed", T)
         pb = wide("pb", LOOKUP_COLS)
+
+        identity = wide("identity", P)
+        make_identity(nc, identity[:])
 
         nc.vector.memset(key_bytes[:].bitcast(I32), 0)
         nc.vector.memset(pb[:, I:], 0.0)
@@ -124,10 +128,12 @@ def tile_attend_hvlinkedproduct_s_kernel(
         dquery_mx = quantise("dquery", dquery_bf16)
         ta = product("ta", dquery_mx, slot_key_words, slot_key_bytes)
 
-        unused = wide("unused", tag="val_bytes")
-        shift = column("shift", "dquery_raw")
-        nc.vector.tensor_scalar(unused[:], a[:], -0.5, None, ALU.mult, ALU.min, accum_out=shift[:])
-        nc.scalar.activation(pb[:, :I], a[:], ACT.Exp, bias=shift[:], scale=0.5)
+        fourth_root = wide("fourth_root")
+        root_sum = column("root_sum", "dquery_raw")
+        nc.scalar.activation(fourth_root[:], a[:], ACT.Exp, scale=0.25, accum_out=root_sum[:])
+        root_scale = column("root_scale", "val_bytes")
+        nc.vector.reciprocal(root_scale[:], root_sum[:])
+        nc.scalar.activation(pb[:, :I], fourth_root[:], ACT.Square, scale=root_scale[:])
         pa = wide("pa")
         nc.scalar.activation(pa[:], pb[:, :I], ACT.Square)
         gout_bf16 = interleave("gout", gout_raw, "val_bytes")
@@ -146,37 +152,52 @@ def tile_attend_hvlinkedproduct_s_kernel(
         nc.vector.scalar_tensor_tensor(tpb[:, :I], ta[:], 0.5, pb[:, :I], ALU.mult, ALU.mult)
         own = wide("own")
         nc.vector.tensor_tensor(own[:], ta[:], p[:], ALU.mult)
-        linked = wide("linked", tag="val_bytes")
-        nc.vector.tensor_tensor(linked[:], tpb[:].indirect(link_list[:]), pa[:], ALU.mult)
         minus_rz = column("minus_rz")
         nc.vector.reciprocal(minus_rz[:], minus_z[:])
+        linked = wide("linked", tag="val_bytes")
+        nc.vector.tensor_tensor(linked[:], tpb[:].indirect(link_list[:]), pa[:], ALU.mult)
         minus_w = wide("minus_w")
         nc.scalar.activation(minus_w[:], p[:], ACT.Copy, scale=minus_rz[:])
         gain = column("gain")
         nc.scalar.activation(gain[:], minus_rz[:], ACT.Copy, scale=-256.0)
 
-        tp = wide("tp")
-        tz = column("tz")
-        nc.vector.scalar_tensor_tensor(tp[:], linked[:], 1.0, own[:], ALU.mult, ALU.add, accum_out=tz[:])
         weighted = wide("weighted")
         minus_mean = column("minus_mean")
         nc.vector.scalar_tensor_tensor(
             weighted[:], c0[:], minus_rz[:], p[:], ALU.mult, ALU.mult, accum_out=minus_mean[:]
         )
+        centred = wide("centred")
+        nc.scalar.activation(centred[:], c0[:], ACT.Identity, bias=minus_mean[:], scale=1.0)
         base_sb = overlaid("base_sb", [P, T], F32, 0)
         nc.sync.dma_start(out=base_sb[:], in_=base)
-        v = wide("v")
-        nc.vector.scalar_tensor_tensor(v[:], minus_w[:], tz[:], tp[:], ALU.mult, ALU.add)
-        cv = wide("cv")
-        cv_sum = column("cv_sum")
-        nc.vector.scalar_tensor_tensor(cv[:], c0[:], minus_mean[:], v[:], ALU.add, ALU.mult, accum_out=cv_sum[:])
-        u = wide("u")
-        nc.vector.scalar_tensor_tensor(u[:], minus_w[:], cv_sum[:], cv[:], ALU.mult, ALU.add)
+        tp = wide("tp")
+        tz = column("tz")
+        nc.vector.scalar_tensor_tensor(tp[:], linked[:], 1.0, own[:], ALU.mult, ALU.add, accum_out=tz[:])
+        centred_tz = wide("centred_tz")
+        nc.scalar.activation(centred_tz[:], centred[:], ACT.Copy, scale=tz[:])
+        moved = wide("moved")
+        moved_sum = column("moved_sum")
+        nc.vector.scalar_tensor_tensor(moved[:], c0[:], minus_mean[:], tp[:], ALU.add, ALU.mult, accum_out=moved_sum[:])
+        kept = wide("kept")
+        nc.vector.scalar_tensor_tensor(kept[:], centred_tz[:], moved_sum[:], minus_w[:], ALU.add, ALU.mult)
 
         sent = wide("sent", LINK_COLS)
-        nc.vector.tensor_copy(sent[:].indirect(link_list[:]), u[:])
+        nc.vector.tensor_tensor(sent[:].indirect(link_list[:]), moved[:], kept[:], ALU.add)
+
+        blocks = [slice(P * b, P * (b + 1)) for b in range(I // P)]
+        turned = [ps.tile([P, P], F32, name="turned%d" % b) for b in range(I // P)]
+        for term, first in ((moved, True), (kept, False)):
+            for b, cols in enumerate(blocks):
+                nc.tensor.matmul(
+                    turned[b][:], lhsT=term[:, cols], rhs=identity[:], start=first, stop=not first, is_transpose=True
+                )
+        back = ps.tile([P, I], F32, name="back")
+        for b, cols in enumerate(blocks):
+            turned_sb = wide("turned_sb%d" % b, P)
+            nc.scalar.copy(out=turned_sb[:], in_=turned[b][:])
+            nc.tensor.transpose(back[:, cols], turned_sb[:], identity[:])
         twice_u = wide("twice_u")
-        nc.scalar.activation(twice_u[:], u[:], ACT.Copy, scale=2.0)
+        nc.scalar.activation(twice_u[:], back[:], ACT.Copy, scale=2.0)
         nc.vector.tensor_tensor(placed[:].indirect(token_list[:]), twice_u[:], sent[:, :I], ALU.add)
 
         for k in range(len(OUT_EDGES) - 1):

@@ -51,13 +51,13 @@ def tile_attend_hvlinkedproduct_s_kernel(
         placed = wide("placed", T)
         pb = wide("pb", LOOKUP_COLS)
 
-        identity = wide("identity", P)
-        make_identity(nc, identity[:])
-
         nc.vector.memset(key_bytes[:].bitcast(I32), 0)
         nc.vector.memset(pb[:, I:], 0.0)
         nc.vector.memset(placed[:], 0.0)
         nc.vector.memset(val_bytes[:].bitcast(I32), 0)
+        identity = wide("identity", P)
+        nc.vector.memset(identity[:], 0.0)
+        make_identity(nc, identity[:], nomemset=True)
 
         def load_scale_rows(tile, rows):
             for quad in range(4):
@@ -91,7 +91,7 @@ def tile_attend_hvlinkedproduct_s_kernel(
             return got
 
         def product(name, stationary, words, scale_bytes):
-            bank = ps.tile([P, I], F32, name=name)
+            bank = ps.tile([P, I], F32, name=name, tag=name)
             nc.tensor.matmul_mx(
                 out=bank[:],
                 lhsT=stationary[0][:].bitcast(FP8X4),
@@ -191,13 +191,14 @@ def tile_attend_hvlinkedproduct_s_kernel(
                 nc.tensor.matmul(
                     turned[b][:], lhsT=term[:, cols], rhs=identity[:], start=first, stop=not first, is_transpose=True
                 )
-        back = ps.tile([P, I], F32, name="back")
-        for b, cols in enumerate(blocks):
-            turned_sb = wide("turned_sb%d" % b, P)
-            nc.scalar.copy(out=turned_sb[:], in_=turned[b][:])
-            nc.tensor.transpose(back[:, cols], turned_sb[:], identity[:])
         twice_u = wide("twice_u")
-        nc.scalar.activation(twice_u[:], back[:], ACT.Copy, scale=2.0)
+        for half, tag in enumerate(("a", "ta")):
+            back = ps.tile([P, I // 2], F32, name="back%d" % half, tag=tag)
+            for j in range(2):
+                turned_sb = wide("turned_sb%d" % (2 * half + j), P)
+                nc.scalar.copy(out=turned_sb[:], in_=turned[2 * half + j][:])
+                nc.tensor.transpose(back[:, blocks[j]], turned_sb[:], identity[:])
+            nc.scalar.activation(twice_u[:, half * I // 2 : (half + 1) * I // 2], back[:], ACT.Copy, scale=2.0)
         nc.vector.tensor_tensor(placed[:].indirect(token_list[:]), twice_u[:], sent[:, :I], ALU.add)
 
         for k in range(len(OUT_EDGES) - 1):

from contextlib import ExitStack

import concourse.mybir as mybir
from concourse.masks import make_identity

D, E, T, I, Q = 512, 512, 2048, 512, 128
FLOPS = 3 * 2 * 512 * Q * I

F32 = mybir.dt.float32
BF16 = mybir.dt.bfloat16
I32 = mybir.dt.int32
U32 = mybir.dt.uint32
U16 = mybir.dt.uint16
U8 = mybir.dt.uint8
FP8X4 = mybir.dt.float8_e4m3fn_x4
ALU = mybir.AluOpType
ACT = mybir.ActivationFunctionType

P = 128
PACK = 4
LOOKUP_COLS = I + 16
LINK_COLS = 2 * I
OUT_EDGES = (0, 256, 768, 1280, 1792, 2048)


def tile_attend_hvlinkedproduct_s_kernel(
    tc, query, keys_words, keys_scales, gout, vals_words, vals_scales, dquery, base, offs2, offs, out
):
    nc = tc.nc
    with ExitStack() as ctx:
        lists = ctx.enter_context(tc.tile_pool(name="lists", bufs=1))
        sb = ctx.enter_context(tc.tile_pool(name="sb", bufs=1))
        shared = ctx.enter_context(tc.tile_pool(name="shared", bufs=1))
        ps = ctx.enter_context(tc.psum_pool(name="ps", bufs=1))

        token_list = lists.tile([P, I // 16], U16, name="token_list")
        link_list = lists.tile([P, I // 16], U16, name="link_list")

        def wide(name, cols=I, dtype=F32, tag=None):
            return sb.tile([P, cols], dtype, name=name, tag=tag or name, align_bytes=64)

        def column(name, tag=None):
            return sb.tile([P, 1], F32, name=name, tag=tag or name, align_bytes=64)

        def overlaid(name, shape, dtype, offset):
            return shared.tile(shape, dtype, name=name, offset=offset, align_bytes=64)

        key_bytes = wide("key_bytes", T, U8)
        val_bytes = wide("val_bytes", T, U8)
        key_words = wide("key_words", T, I32)
        placed = wide("placed", T)
        pb = wide("pb", LOOKUP_COLS)

        nc.vector.memset(key_bytes[:].bitcast(I32), 0)
        nc.vector.memset(pb[:, I:], 0.0)
        nc.vector.memset(placed[:], 0.0)
        nc.vector.memset(val_bytes[:].bitcast(I32), 0)
        identity = wide("identity", P)
        nc.vector.memset(identity[:], 0.0)
        make_identity(nc, identity[:], nomemset=True)

        def load_scale_rows(tile, rows):
            for quad in range(4):
                nc.sync.dma_start(
                    out=tile[32 * quad : 32 * quad + 4, :].bitcast(I32),
                    in_=rows[0, 4 * quad : 4 * quad + 4, :].bitcast(I32),
                )

        def load_words(tile, words):
            nc.sync.dma_start(out=tile[:], in_=words[0].rearrange("p n t -> p (n t)").bitcast(I32))

        def load_rows(raw, rows):
            nc.sync.dma_start(out=raw[:], in_=rows.rearrange("(p j) w -> p j w", j=PACK))

        def interleave(name, raw, tag):
            grouped = sb.tile([P, Q, PACK], BF16, name=name + "_bf16", tag=tag, align_bytes=64)
            nc.scalar.copy(out=grouped[:], in_=raw[:].rearrange("p j w -> p w j"))
            return grouped

        def quantise(name, grouped):
            codes = wide(name + "_codes", Q, U32)
            scales = wide(name + "_scales", Q, U8)
            nc.vector.quantize_mx(
                out=codes[:].bitcast(FP8X4), scales=scales[:], in_=grouped[:].rearrange("p w j -> p (w j)")
            )
            return codes, scales

        def gather(name, window):
            got = wide(name, I, window.dtype)
            nc.vector.tensor_copy(got[:], window.indirect(token_list[:]))
            return got

        def product(name, stationary, words, scale_bytes):
            bank = ps.tile([P, I], F32, name=name, tag=name)
            nc.tensor.matmul_mx(
                out=bank[:],
                lhsT=stationary[0][:].bitcast(FP8X4),
                lhsT_scale=stationary[1][:],
                rhs=words[:].bitcast(FP8X4),
                rhs_scale=scale_bytes[:],
                start=True,
                stop=True,
            )
            return bank

        nc.sync.dma_start(token_list[:], offs)
        nc.sync.dma_start(link_list[:], offs2)
        query_raw = overlaid("query_raw", [P, PACK, Q], F32, 0)
        load_rows(query_raw, query)
        load_scale_rows(key_bytes, keys_scales)
        load_words(key_words, keys_words)
        dquery_raw = sb.tile([P, PACK, Q], F32, name="dquery_raw", tag="dquery_raw", align_bytes=64)
        load_rows(dquery_raw, dquery)
        load_scale_rows(val_bytes, vals_scales)

        query_bf16 = interleave("query", query_raw, "query_bf16")
        val_words = overlaid("val_words", [P, T], I32, 0)
        load_words(val_words, vals_words)
        dquery_bf16 = interleave("dquery", dquery_raw, "dquery_bf16")

        slot_key_bytes = gather("slot_key_bytes", key_bytes[:])
        gout_raw = sb.tile([P, PACK, Q], F32, name="gout_raw", tag="key_bytes", align_bytes=64)
        load_rows(gout_raw, gout)
        query_mx = quantise("query", query_bf16)
        slot_key_words = gather("slot_key_words", key_words[:].bitcast(U32))
        a = product("a", query_mx, slot_key_words, slot_key_bytes)
        slot_val_bytes = gather("slot_val_bytes", val_bytes[:])
        dquery_mx = quantise("dquery", dquery_bf16)
        ta = product("ta", dquery_mx, slot_key_words, slot_key_bytes)

        fourth_root = wide("fourth_root")
        root_sum = column("root_sum", "dquery_raw")
        nc.scalar.activation(fourth_root[:], a[:], ACT.Exp, scale=0.25, accum_out=root_sum[:])
        root_scale = column("root_scale", "val_bytes")
        nc.vector.reciprocal(root_scale[:], root_sum[:])
        nc.scalar.activation(pb[:, :I], fourth_root[:], ACT.Square, scale=root_scale[:])
        pa = wide("pa")
        nc.scalar.activation(pa[:], pb[:, :I], ACT.Square)
        gout_bf16 = interleave("gout", gout_raw, "val_bytes")

        slot_val_words = gather("slot_val_words", val_words[:].bitcast(U32))
        p = overlaid("p", [P, I], F32, 0)
        nc.vector.tensor_tensor(p[:], pb[:].indirect(link_list[:]), pa[:], ALU.mult)
        minus_p = wide("minus_p")
        minus_z = column("minus_z")
        nc.scalar.activation(minus_p[:], p[:], ACT.Copy, scale=-1.0, accum_out=minus_z[:])
        gout_mx = quantise("gout", gout_bf16)
        c0 = product("c0", gout_mx, slot_val_words, slot_val_bytes)

        tpb = overlaid("tpb", [P, LOOKUP_COLS], F32, 4 * I)
        nc.vector.memset(tpb[:, I:], 0.0)
        nc.vector.scalar_tensor_tensor(tpb[:, :I], ta[:], 0.5, pb[:, :I], ALU.mult, ALU.mult)
        own = wide("own")
        nc.vector.tensor_tensor(own[:], ta[:], p[:], ALU.mult)
        minus_rz = column("minus_rz")
        nc.vector.reciprocal(minus_rz[:], minus_z[:])
        linked = wide("linked", tag="val_bytes")
        nc.vector.tensor_tensor(linked[:], tpb[:].indirect(link_list[:]), pa[:], ALU.mult)
        minus_w = wide("minus_w")
        nc.scalar.activation(minus_w[:], p[:], ACT.Copy, scale=minus_rz[:])
        gain = column("gain")
        nc.scalar.activation(gain[:], minus_rz[:], ACT.Copy, scale=-256.0)

        weighted = wide("weighted")
        minus_mean = column("minus_mean")
        nc.vector.scalar_tensor_tensor(
            weighted[:], c0[:], minus_rz[:], p[:], ALU.mult, ALU.mult, accum_out=minus_mean[:]
        )
        centred = wide("centred")
        nc.scalar.activation(centred[:], c0[:], ACT.Identity, bias=minus_mean[:], scale=1.0)
        base_sb = overlaid("base_sb", [P, T], F32, 0)
        nc.sync.dma_start(out=base_sb[:], in_=base)
        tp = wide("tp")
        tz = column("tz")
        nc.vector.scalar_tensor_tensor(tp[:], linked[:], 1.0, own[:], ALU.mult, ALU.add, accum_out=tz[:])
        centred_tz = wide("centred_tz")
        nc.scalar.activation(centred_tz[:], centred[:], ACT.Copy, scale=tz[:])
        moved = wide("moved")
        moved_sum = column("moved_sum")
        nc.vector.scalar_tensor_tensor(moved[:], c0[:], minus_mean[:], tp[:], ALU.add, ALU.mult, accum_out=moved_sum[:])
        kept = wide("kept")
        nc.vector.scalar_tensor_tensor(kept[:], centred_tz[:], moved_sum[:], minus_w[:], ALU.add, ALU.mult)

        sent = wide("sent", LINK_COLS)
        nc.vector.tensor_tensor(sent[:].indirect(link_list[:]), moved[:], kept[:], ALU.add)

        blocks = [slice(P * b, P * (b + 1)) for b in range(I // P)]
        turned = [ps.tile([P, P], F32, name="turned%d" % b) for b in range(I // P)]
        for term, first in ((moved, True), (kept, False)):
            for b, cols in enumerate(blocks):
                nc.tensor.matmul(
                    turned[b][:], lhsT=term[:, cols], rhs=identity[:], start=first, stop=not first, is_transpose=True
                )
        twice_u = wide("twice_u")
        for half, tag in enumerate(("a", "ta")):
            back = ps.tile([P, I // 2], F32, name="back%d" % half, tag=tag)
            for j in range(2):
                turned_sb = wide("turned_sb%d" % (2 * half + j), P)
                nc.scalar.copy(out=turned_sb[:], in_=turned[2 * half + j][:])
                nc.tensor.transpose(back[:, blocks[j]], turned_sb[:], identity[:])
            nc.scalar.activation(twice_u[:, half * I // 2 : (half + 1) * I // 2], back[:], ACT.Copy, scale=2.0)
        nc.vector.tensor_tensor(placed[:].indirect(token_list[:]), twice_u[:], sent[:, :I], ALU.add)

        for k in range(len(OUT_EDGES) - 1):
            cols = slice(OUT_EDGES[k], OUT_EDGES[k + 1])
            result = wide("result%d" % k, cols.stop - cols.start)
            nc.vector.scalar_tensor_tensor(result[:], placed[:, cols], gain[:], base_sb[:, cols], ALU.mult, ALU.add)
            queue = nc.sync if k % 2 == 0 else nc.scalar
            queue.dma_start(out=out[:, cols], in_=result[:])
